import numpy as np
import ml_dtypes

BF16 = ml_dtypes.bfloat16


def bf(x):
    return np.asarray(x, np.float32).astype(BF16)


def f32(x):
    return np.asarray(x, np.float32)


def f64(x):
    return np.asarray(x).astype(np.float64)


def striped(idx):
    return np.tile(idx.reshape(-1, 16).T, (8, 1))


def rows(idx, k):
    return np.tile(idx, (k, 1))


def look(tab, idx):
    return np.take_along_axis(f64(tab), rows(idx, len(tab)), axis=1)


K, S, V, N, M = 256, 2048, 512, 512, 512


def setup_inputs():
    return {"tab": f32(np.random.standard_normal((2, K, S))), "y": f32(np.random.standard_normal((K, V))), "w": bf(np.random.standard_normal((K, M)) / np.sqrt(K)), "b": f32(0.5 * np.random.standard_normal((M, 1))), "offs": striped(np.random.permutation(S)[:N])}


def reference(tab, y, w, b, offs):
    idx = offs[:16].T.reshape(-1)
    x = (look(tab[0], idx) - f64(y)) * (np.tanh(look(tab[1], idx)))
    return np.maximum(f64(w).T @ x + f64(b), 0.0)

@@ -1,0 +1,71 @@
+import concourse.mybir as mybir
+
+F32, BF16, U16 = mybir.dt.float32, mybir.dt.bfloat16, mybir.dt.uint16
+ALU = mybir.AluOpType
+ACT = mybir.ActivationFunctionType
+
+P = 128
+R, S = 256, 2048
+N, M = 512, 512
+C = R // P
+G = M // P
+
+FLOPS = 2 * M * N * R
+
+
+def tile_lookup_vg_subtanh_relu_kernel(tc, tab, y, w, b, offs, out):
+    nc = tc.nc
+    tables = tab.rearrange("t (p c) s -> t c p s", c=C)
+    y_rows = y.rearrange("(p c) n -> p (c n)", c=C)
+    w_rows = w.rearrange("(p c) m -> p (c m)", c=C)
+    b_rows = b.rearrange("(p g) one -> p (g one)", g=G)
+    out_rows = out.rearrange("(p g) n -> g p n", g=G)
+
+    with (
+        tc.tile_pool(name="held", bufs=1) as held,
+        tc.psum_pool(name="psum", bufs=1) as psum,
+    ):
+        offsets = held.tile([P, N // 16], U16, name="offsets")
+        nc.sync.dma_start(offsets[:], offs)
+
+        values = [held.tile([P, S], F32, name=f"values{c}") for c in range(C)]
+        gates = [held.tile([P, S], F32, name=f"gates{c}") for c in range(C)]
+        y_tile = held.tile([P, C * N], F32, name="y_tile")
+        w_tile = held.tile([P, C * M], BF16, name="w_tile")
+        b_tile = held.tile([P, G], F32, name="b_tile")
+
+        nc.sync.dma_start(values[0][:], tables[0, 0])
+        nc.sync.dma_start(y_tile[:], y_rows)
+        nc.sync.dma_start(gates[0][:], tables[1, 0])
+        nc.sync.dma_start(w_tile[:], w_rows)
+        nc.sync.dma_start(b_tile[:], b_rows)
+        nc.sync.dma_start(values[1][:], tables[0, 1])
+        nc.sync.dma_start(gates[1][:], tables[1, 1])
+
+        sums = [psum.tile([P, N], F32, name=f"sums{g}") for g in range(G)]
+        for c in range(C):
+            diff = held.tile([P, N], F32, name=f"diff{c}")
+            nc.vector.tensor_tensor(
+                diff[:], values[c][:].indirect(offsets[:]), y_tile[:, c * N : (c + 1) * N], ALU.subtract
+            )
+            gate = held.tile([P, N], F32, name=f"gate{c}")
+            nc.scalar.activation(gate[:], gates[c][:].indirect(offsets[:]), ACT.Tanh)
+            x = held.tile([P, N], BF16, name=f"x{c}")
+            nc.vector.tensor_tensor(x[:], diff[:], gate[:], ALU.mult)
+            for g in range(G):
+                nc.tensor.matmul(
+                    sums[g][:],
+                    w_tile[:, c * M + g : (c + 1) * M : G],
+                    x[:],
+                    start=(c == 0),
+                    stop=(c == C - 1),
+                )
+
+        for g in range(G):
+            result = held.tile([P, N], F32, name=f"result{g}")
+            bias = b_tile[:, g : g + 1]
+            if g % 2 == 0:
+                nc.vector.tensor_scalar(result[:], sums[g][:], bias, 0.0, ALU.add, ALU.max)
+            else:
+                nc.scalar.activation(result[:], sums[g][:], ACT.Relu, bias=bias)
+            nc.sync.dma_start(out_rows[g], result[:])

@@ -10,6 +10,9 @@ N, M = 512, 512
 C = R // P
 G = M // P
 
+HALVES = 2
+HALF = N // HALVES
+
 FLOPS = 2 * M * N * R
 
 
@@ -36,36 +39,47 @@ def tile_lookup_vg_subtanh_relu_kernel(tc, tab, y, w, b, offs, out):
 
         nc.sync.dma_start(values[0][:], tables[0, 0])
         nc.sync.dma_start(y_tile[:], y_rows)
+        nc.sync.dma_start(values[1][:], tables[0, 1])
         nc.sync.dma_start(gates[0][:], tables[1, 0])
         nc.sync.dma_start(w_tile[:], w_rows)
         nc.sync.dma_start(b_tile[:], b_rows)
-        nc.sync.dma_start(values[1][:], tables[0, 1])
         nc.sync.dma_start(gates[1][:], tables[1, 1])
 
-        sums = [psum.tile([P, N], F32, name=f"sums{g}") for g in range(G)]
-        for c in range(C):
-            diff = held.tile([P, N], F32, name=f"diff{c}")
-            nc.vector.tensor_tensor(
-                diff[:], values[c][:].indirect(offsets[:]), y_tile[:, c * N : (c + 1) * N], ALU.subtract
-            )
-            gate = held.tile([P, N], F32, name=f"gate{c}")
-            nc.scalar.activation(gate[:], gates[c][:].indirect(offsets[:]), ACT.Tanh)
-            x = held.tile([P, N], BF16, name=f"x{c}")
-            nc.vector.tensor_tensor(x[:], diff[:], gate[:], ALU.mult)
-            for g in range(G):
-                nc.tensor.matmul(
-                    sums[g][:],
-                    w_tile[:, c * M + g : (c + 1) * M : G],
-                    x[:],
-                    start=(c == 0),
-                    stop=(c == C - 1),
-                )
+        zero = held.tile([P, 1], F32, name="zero")
+        nc.vector.memset(zero[:], 0.0)
+        tanh_of_zero = held.tile([P, 1], F32, name="tanh_of_zero")
+        nc.scalar.activation(tanh_of_zero[:], zero[:], ACT.Tanh)
 
-        for g in range(G):
-            result = held.tile([P, N], F32, name=f"result{g}")
-            bias = b_tile[:, g : g + 1]
-            if g % 2 == 0:
-                nc.vector.tensor_scalar(result[:], sums[g][:], bias, 0.0, ALU.add, ALU.max)
-            else:
-                nc.scalar.activation(result[:], sums[g][:], ACT.Relu, bias=bias)
-            nc.sync.dma_start(out_rows[g], result[:])
+        sums = [[psum.tile([P, HALF], F32, name=f"sums{h}_{g}") for g in range(G)] for h in range(HALVES)]
+        diffs = [held.tile([P, N], F32, name=f"diff{c}") for c in range(C)]
+        for c in range(C):
+            nc.vector.tensor_tensor(
+                diffs[c][:], values[c][:].indirect(offsets[:]), y_tile[:, c * N : (c + 1) * N], ALU.subtract
+            )
+        for c in range(C):
+            for h in range(HALVES):
+                piece = slice(h * HALF, (h + 1) * HALF)
+                gate = held.tile([P, HALF], F32, name=f"gate{c}_{h}")
+                nc.scalar.activation(
+                    gate[:], gates[c][:].indirect(offsets[:, h * HALF // 16 : (h + 1) * HALF // 16]), ACT.Tanh
+                )
+                x = held.tile([P, HALF], BF16, name=f"x{c}_{h}")
+                nc.vector.tensor_tensor(x[:], diffs[c][:, piece], gate[:], ALU.mult)
+                for g in range(G):
+                    nc.tensor.matmul(
+                        sums[h][g][:],
+                        w_tile[:, c * M + g : (c + 1) * M : G],
+                        x[:],
+                        start=(c == 0),
+                        stop=(c == C - 1),
+                    )
+
+        for h in range(HALVES):
+            for g in range(G):
+                result = held.tile([P, HALF], F32, name=f"result{h}_{g}")
+                bias = b_tile[:, g : g + 1]
+                if g % 2 == 0:
+                    nc.vector.tensor_scalar(result[:], sums[h][g][:], bias, 0.0, ALU.add, ALU.max)
+                else:
+                    nc.scalar.activation(result[:], sums[h][g][:], ACT.Relu, bias=bias)
+                nc.sync.dma_start(out_rows[g, :, h * HALF : (h + 1) * HALF], result[:])

@@ -38,11 +38,11 @@ def tile_lookup_vg_subtanh_relu_kernel(tc, tab, y, w, b, offs, out):
         b_tile = held.tile([P, G], F32, name="b_tile")
 
         nc.sync.dma_start(values[0][:], tables[0, 0])
-        nc.sync.dma_start(y_tile[:], y_rows)
+        nc.scalar.dma_start(y_tile[:], y_rows)
         nc.sync.dma_start(values[1][:], tables[0, 1])
-        nc.sync.dma_start(gates[0][:], tables[1, 0])
-        nc.sync.dma_start(w_tile[:], w_rows)
-        nc.sync.dma_start(b_tile[:], b_rows)
+        nc.scalar.dma_start(gates[0][:], tables[1, 0])
+        nc.scalar.dma_start(w_tile[:], w_rows)
+        nc.scalar.dma_start(b_tile[:], b_rows)
         nc.sync.dma_start(gates[1][:], tables[1, 1])
 
         zero = held.tile([P, 1], F32, name="zero")

@@ -20,7 +20,7 @@ def tile_lookup_vg_subtanh_relu_kernel(tc, tab, y, w, b, offs, out):
     nc = tc.nc
     tables = tab.rearrange("t (p c) s -> t c p s", c=C)
     y_rows = y.rearrange("(p c) n -> p (c n)", c=C)
-    w_rows = w.rearrange("(p c) m -> p (c m)", c=C)
+    w_rows = w.rearrange("(p c) m -> c p m", c=C)
     b_rows = b.rearrange("(p g) one -> p (g one)", g=G)
     out_rows = out.rearrange("(p g) n -> g p n", g=G)
 
@@ -34,16 +34,17 @@ def tile_lookup_vg_subtanh_relu_kernel(tc, tab, y, w, b, offs, out):
         values = [held.tile([P, S], F32, name=f"values{c}") for c in range(C)]
         gates = [held.tile([P, S], F32, name=f"gates{c}") for c in range(C)]
         y_tile = held.tile([P, C * N], F32, name="y_tile")
-        w_tile = held.tile([P, C * M], BF16, name="w_tile")
+        w_tiles = [held.tile([P, M], BF16, name=f"w_tile{c}") for c in range(C)]
         b_tile = held.tile([P, G], F32, name="b_tile")
 
         nc.sync.dma_start(values[0][:], tables[0, 0])
         nc.scalar.dma_start(y_tile[:], y_rows)
         nc.sync.dma_start(values[1][:], tables[0, 1])
         nc.scalar.dma_start(gates[0][:], tables[1, 0])
-        nc.scalar.dma_start(w_tile[:], w_rows)
-        nc.scalar.dma_start(b_tile[:], b_rows)
+        nc.scalar.dma_start(w_tiles[0][:], w_rows[0])
         nc.sync.dma_start(gates[1][:], tables[1, 1])
+        nc.sync.dma_start(w_tiles[1][:], w_rows[1])
+        nc.sync.dma_start(b_tile[:], b_rows)
 
         zero = held.tile([P, 1], F32, name="zero")
         nc.vector.memset(zero[:], 0.0)
@@ -68,7 +69,7 @@ def tile_lookup_vg_subtanh_relu_kernel(tc, tab, y, w, b, offs, out):
                 for g in range(G):
                     nc.tensor.matmul(
                         sums[h][g][:],
-                        w_tile[:, c * M + g : (c + 1) * M : G],
+                        w_tiles[c][:, g::G],
                         x[:],
                         start=(c == 0),
                         stop=(c == C - 1),

import concourse.mybir as mybir

F32, BF16, U16 = mybir.dt.float32, mybir.dt.bfloat16, mybir.dt.uint16
ALU = mybir.AluOpType
ACT = mybir.ActivationFunctionType

P = 128
R, S = 256, 2048
N, M = 512, 512
C = R // P
G = M // P

HALVES = 2
HALF = N // HALVES

FLOPS = 2 * M * N * R


def tile_lookup_vg_subtanh_relu_kernel(tc, tab, y, w, b, offs, out):
    nc = tc.nc
    tables = tab.rearrange("t (p c) s -> t c p s", c=C)
    y_rows = y.rearrange("(p c) n -> p (c n)", c=C)
    w_rows = w.rearrange("(p c) m -> c p m", c=C)
    b_rows = b.rearrange("(p g) one -> p (g one)", g=G)
    out_rows = out.rearrange("(p g) n -> g p n", g=G)

    with (
        tc.tile_pool(name="held", bufs=1) as held,
        tc.psum_pool(name="psum", bufs=1) as psum,
    ):
        offsets = held.tile([P, N // 16], U16, name="offsets")
        nc.sync.dma_start(offsets[:], offs)

        values = [held.tile([P, S], F32, name=f"values{c}") for c in range(C)]
        gates = [held.tile([P, S], F32, name=f"gates{c}") for c in range(C)]
        y_tile = held.tile([P, C * N], F32, name="y_tile")
        w_tiles = [held.tile([P, M], BF16, name=f"w_tile{c}") for c in range(C)]
        b_tile = held.tile([P, G], F32, name="b_tile")

        nc.sync.dma_start(values[0][:], tables[0, 0])
        nc.scalar.dma_start(y_tile[:], y_rows)
        nc.sync.dma_start(values[1][:], tables[0, 1])
        nc.scalar.dma_start(gates[0][:], tables[1, 0])
        nc.scalar.dma_start(w_tiles[0][:], w_rows[0])
        nc.sync.dma_start(gates[1][:], tables[1, 1])
        nc.sync.dma_start(w_tiles[1][:], w_rows[1])
        nc.sync.dma_start(b_tile[:], b_rows)

        zero = held.tile([P, 1], F32, name="zero")
        nc.vector.memset(zero[:], 0.0)
        tanh_of_zero = held.tile([P, 1], F32, name="tanh_of_zero")
        nc.scalar.activation(tanh_of_zero[:], zero[:], ACT.Tanh)

        sums = [[psum.tile([P, HALF], F32, name=f"sums{h}_{g}") for g in range(G)] for h in range(HALVES)]
        diffs = [held.tile([P, N], F32, name=f"diff{c}") for c in range(C)]
        for c in range(C):
            nc.vector.tensor_tensor(
                diffs[c][:], values[c][:].indirect(offsets[:]), y_tile[:, c * N : (c + 1) * N], ALU.subtract
            )
        for c in range(C):
            for h in range(HALVES):
                piece = slice(h * HALF, (h + 1) * HALF)
                gate = held.tile([P, HALF], F32, name=f"gate{c}_{h}")
                nc.scalar.activation(
                    gate[:], gates[c][:].indirect(offsets[:, h * HALF // 16 : (h + 1) * HALF // 16]), ACT.Tanh
                )
                x = held.tile([P, HALF], BF16, name=f"x{c}_{h}")
                nc.vector.tensor_tensor(x[:], diffs[c][:, piece], gate[:], ALU.mult)
                for g in range(G):
                    nc.tensor.matmul(
                        sums[h][g][:],
                        w_tiles[c][:, g::G],
                        x[:],
                        start=(c == 0),
                        stop=(c == C - 1),
                    )

        for h in range(HALVES):
            for g in range(G):
                result = held.tile([P, HALF], F32, name=f"result{h}_{g}")
                bias = b_tile[:, g : g + 1]
                if g % 2 == 0:
                    nc.vector.tensor_scalar(result[:], sums[h][g][:], bias, 0.0, ALU.add, ALU.max)
                else:
                    nc.scalar.activation(result[:], sums[h][g][:], ACT.Relu, bias=bias)
                nc.sync.dma_start(out_rows[g, :, h * HALF : (h + 1) * HALF], result[:])
